import numpy as np
import ml_dtypes


def mxq(x, axis, fmt="e4m3"):
    dtype, down = {"e4m3": (ml_dtypes.float8_e4m3fn, 7), "e5m2": (ml_dtypes.float8_e5m2, 14)}[fmt]
    v = np.moveaxis(np.asarray(x, np.float32).astype(ml_dtypes.bfloat16).astype(np.float64), axis, -1)
    blocks = v.reshape(v.shape[:-1] + (-1, 32))
    amax = np.abs(blocks).max(-1, keepdims=True)
    byte = np.maximum(np.where(amax > 0, np.frexp(amax)[1] - 1 + 127, 0) - down, 1)
    scale = np.exp2(byte - 127.0)
    codes = (blocks / scale).astype(np.float32).astype(dtype).astype(np.float64)
    return np.moveaxis((codes * scale).reshape(v.shape), -1, axis)


WIDE = False


def mx_kscale(k):
    if not WIDE:
        return np.ones(k)
    levels = np.array([10, -10, 5, -5, 0])
    if k % 512:
        return np.exp2(np.random.permutation(np.resize(levels, k // 32))).repeat(32)
    a = np.empty((k // 512, 16))
    for p in range(k // 512):
        a[p, :8] = np.random.permutation(np.resize(levels, 8))
        for g in range(8):
            far = levels[np.abs(levels - a[p, g]) >= 10]
            a[p, g + 8] = far[np.random.randint(len(far))]
    return np.exp2(a.ravel()).repeat(32)


def f64(x):
    return np.asarray(x).astype(np.float64)


def striped(idx):
    return np.tile(idx.reshape(-1, 16).T, (8, 1)).astype(np.uint16)


def unstriped(offs):
    return offs[:16].T.reshape(-1).astype(np.int64)


E2M1 = np.array([0.0, 0.5, 1.0, 1.5, 2.0, 3.0, 4.0, 6.0, -0.0, -0.5, -1.0, -1.5, -2.0, -3.0, -4.0, -6.0])


def pack_weight(w, fmt):
    k, n = w.shape
    w = f64(np.asarray(w, np.float32).astype(ml_dtypes.bfloat16)).reshape(k // 32, 32, n)
    amax = np.abs(w).max(1)
    if fmt == "e4m3":
        byte = np.frexp(amax)[1] - 1 + 127 - 7
    else:
        mant, ex = np.frexp(amax / 6.0)
        byte = np.where(mant > 0.5, ex, ex - 1) + 127
    byte = np.clip(np.where(amax > 0, byte, 1), 1, 254)
    scaled = (w * np.exp2(127.0 - byte)[:, None, :]).reshape(k, n).astype(np.float32)
    by_word = np.ascontiguousarray(scaled.reshape(k // 512, 128, 4, n).transpose(0, 1, 3, 2))
    if fmt == "e4m3":
        words = by_word.astype(ml_dtypes.float8_e4m3fn).view(np.uint8)
    else:
        c = by_word.astype(ml_dtypes.float4_e2m1fn).view(np.uint8) & 0xF
        words = (c[..., 0::2] | (c[..., 1::2] << 4)).reshape(k // 512, 128, 2 * n)
    return np.ascontiguousarray(words), np.ascontiguousarray(byte.astype(np.uint8).reshape(k // 512, 16, n))


def unpack_weight(words, scales, fmt):
    g, _, n = scales.shape
    words = np.ascontiguousarray(words).reshape(g, 128, n, -1)
    if fmt == "e4m3":
        vals = words.view(ml_dtypes.float8_e4m3fn).astype(np.float64)
    else:
        nib = np.empty((g, 128, n, 4), np.uint8)
        nib[..., 0::2] = words & 0xF
        nib[..., 1::2] = words >> 4
        vals = E2M1[nib]
    vals = vals * np.repeat(np.exp2(scales.astype(np.float64) - 127.0), 8, axis=1)[..., None]
    return vals.transpose(0, 1, 3, 2).reshape(g * 512, n)


def silu(v):
    return v / (1.0 + np.exp(-np.maximum(v, -700.0)))


K, L, T, Q, E, C, D = 1024, 512, 768, 1024, 4, 128, 256
H, N = 512, 256


def by_expert(wq, xq, C):
    return np.concatenate([wq[e].T @ xq[:, e * C:(e + 1) * C] for e in range(E)], axis=1)


def setup_inputs():
    n = np.random.standard_normal
    s = mx_kscale(K)
    v = mx_kscale(L)
    u = mx_kscale(H)
    slots1, slots2 = np.random.permutation(T)[:E * C], np.random.permutation(Q)[:E * D]
    x = pack_weight(n((K, T)) * s[:, None], "e4m3")
    z = pack_weight(n((L, Q)) * v[:, None], "e4m3")
    w1 = [pack_weight(m, "e2m1") for m in n((E, K, H)) / np.sqrt(K) / s[None, :, None] * u]
    wz = [pack_weight(m, "e2m1") for m in n((E, L, H)) / np.sqrt(L) / v[None, :, None] * u]
    w2 = [pack_weight(m, "e2m1") for m in n((E, H, N)) / np.sqrt(H) / u[None, :, None]]
    return {
        "x_words": x[0],
        "x_scales": x[1],
        "z_words": z[0],
        "z_scales": z[1],
        "w1_words": np.stack([m[0] for m in w1]),
        "w1_scales": np.stack([m[1] for m in w1]),
        "wz_words": np.stack([m[0] for m in wz]),
        "wz_scales": np.stack([m[1] for m in wz]),
        "w2_words": np.stack([m[0] for m in w2]),
        "w2_scales": np.stack([m[1] for m in w2]),
        "gate1": (np.tile(np.random.uniform(0.2, 1.0, E * C), (128, 1))).astype(np.float32),
        "gate2": (np.tile(np.random.uniform(0.2, 1.0, E * D), (128, 1))).astype(np.float32),
        "offs": striped(slots1),
        "offs2": striped(slots2),
    }


def reference(x_words, x_scales, z_words, z_scales, w1_words, w1_scales, wz_words, wz_scales, w2_words, w2_scales, gate1, gate2, offs, offs2):
    w1 = np.stack([unpack_weight(w1_words[e], w1_scales[e], "e2m1") for e in range(E)])
    wz = np.stack([unpack_weight(wz_words[e], wz_scales[e], "e2m1") for e in range(E)])
    w2 = np.stack([unpack_weight(w2_words[e], w2_scales[e], "e2m1") for e in range(E)])
    idx, idx2 = unstriped(offs), unstriped(offs2)
    xq = unpack_weight(x_words, x_scales, "e4m3")[:, idx]
    zq = unpack_weight(z_words, z_scales, "e4m3")[:, idx2]
    h = silu(by_expert(w1, xq, C))
    p = silu(by_expert(wz, zq, D))
    out = np.zeros((N, T + Q))
    out[:, idx] = f64(gate1[:1]) * by_expert(w2, mxq(h, 0, "e4m3"), C)
    out[:, T + idx2] = f64(gate2[:1]) * by_expert(w2, mxq(p, 0, "e4m3"), D)
    return out

@@ -1,0 +1,210 @@
+from contextlib import ExitStack
+
+import concourse.mybir as mybir
+from concourse.masks import make_identity
+
+K, L, T, Q, E, C, D = 1024, 512, 768, 1024, 4, 128, 256
+H, N = 512, 256
+FLOPS = 2 * E * (C * K * H + D * L * H + (C + D) * H * N)
+
+F32 = mybir.dt.float32
+BF16 = mybir.dt.bfloat16
+I32 = mybir.dt.int32
+U32 = mybir.dt.uint32
+U16 = mybir.dt.uint16
+U8 = mybir.dt.uint8
+FP8X4 = mybir.dt.float8_e4m3fn_x4
+FP4X4 = mybir.dt.float4_e2m1fn_x4
+SILU = mybir.ActivationFunctionType.Silu
+MULT = mybir.AluOpType.mult
+
+P = 128
+UNIT = 256
+PER_COL = 16
+
+
+def tile_moe_mmo_silu_kernel(
+    tc, x_words, x_scales, z_words, z_scales, w1_words, w1_scales, wz_words, wz_scales,
+    w2_words, w2_scales, gate1, gate2, offs, offs2, out,
+):
+    nc = tc.nc
+    with ExitStack() as ctx:
+        keep = ctx.enter_context(tc.tile_pool(name="keep", bufs=1))
+        ring = ctx.enter_context(tc.tile_pool(name="ring", bufs=2))
+        ps1 = ctx.enter_context(tc.psum_pool(name="ps1", bufs=4))
+        pst = ctx.enter_context(tc.psum_pool(name="pst", bufs=2))
+        ps2 = ctx.enter_context(tc.psum_pool(name="ps2", bufs=2))
+
+        def plane(engine, name, width):
+            t = keep.tile([P, width], U8, name=name, tag=name, align_bytes=64)
+            engine.memset(t[:].bitcast(I32), 0)
+            return t
+
+        def load_scale_rows(queue, t, rows):
+            groups = rows.shape[1]
+            for q in range(4):
+                queue.dma_start(
+                    out=t[32 * q : 32 * q + 4, :].bitcast(I32).rearrange("p (g c) -> p g c", g=groups),
+                    in_=rows[4 * q : 4 * q + 4, :, :].bitcast(I32),
+                )
+
+        def load_words(name, tag, src, groups, width):
+            t = keep.tile([P, groups * width], U8, name=name, tag=tag, align_bytes=64)
+            nc.sync.dma_start(
+                out=t[:].bitcast(I32).rearrange("p (g c) -> p g c", g=groups), in_=src.bitcast(I32)
+            )
+            return t
+
+        zs_tab = plane(nc.gpsimd, "zs_tab", Q)
+        wz_pl = plane(nc.vector, "wz_pl", E * H)
+        xs_tab = plane(nc.vector, "xs_tab", T)
+        w2_pl = plane(nc.vector, "w2_pl", E * N)
+        w1_pl = plane(nc.vector, "w1_pl", 2 * E * H)
+        xs1 = plane(nc.vector, "xs1", E * C)
+        text_out = [keep.tile([P, T], F32, name="text_out%d" % b) for b in range(2)]
+        patch_out = [keep.tile([P, Q], F32, name="patch_out%d" % b) for b in range(2)]
+        ident = keep.tile([P, P], F32, name="ident")
+        make_identity(nc, ident[:])
+        for b in range(2):
+            nc.gpsimd.memset(text_out[b][:], 0.0)
+
+        list2 = keep.tile([P, E * D // PER_COL], U16, name="list2")
+        nc.sync.dma_start(list2[:], offs2)
+        zw_tab = keep.tile([P, Q], U32, name="zw_tab", tag="zw_tab", align_bytes=64)
+        nc.sync.dma_start(out=zw_tab[:].bitcast(I32), in_=z_words[0].rearrange("p t d -> p (t d)").bitcast(I32))
+        load_scale_rows(nc.sync, zs_tab, z_scales.rearrange("s b t -> b s t"))
+        wz = load_words("wz", "wz", wz_words.rearrange("e s p c -> p (e s) c"), E, 2 * H)
+        list1 = keep.tile([P, E * C // PER_COL], U16, name="list1")
+        nc.sync.dma_start(list1[:], offs)
+        load_scale_rows(nc.sync, wz_pl, wz_scales.rearrange("e s b i -> b (e s) i"))
+        xw_tab = [keep.tile([P, T], U32, name="xw_tab%d" % s, tag="xw_tab%d" % s, align_bytes=64) for s in range(2)]
+        for s in range(2):
+            nc.sync.dma_start(
+                out=xw_tab[s][:].bitcast(I32), in_=x_words[s].rearrange("p t d -> p (t d)").bitcast(I32)
+            )
+        w2 = load_words("w2", "w2", w2_words.rearrange("e s p c -> p (e s) c"), E, 2 * N)
+        for q in range(4):
+            nc.sync.dma_start(
+                out=xs_tab[32 * q : 32 * q + 8, :].bitcast(I32),
+                in_=x_scales[:, 4 * q : 4 * q + 4, :].bitcast(I32),
+            )
+        load_scale_rows(nc.sync, w2_pl, w2_scales.rearrange("e s b n -> b (e s) n"))
+        load_scale_rows(nc.sync, w1_pl, w1_scales.rearrange("e s b i -> b (e s) i"))
+
+        cols = UNIT // PER_COL
+        zw, zs = [], []
+
+        def gather_patches(u):
+            offsets = list2[:, u * cols : (u + 1) * cols]
+            zw.append(ring.tile([P, UNIT], U32, name="zw", align_bytes=64))
+            nc.vector.tensor_copy(zw[u][:], zw_tab[:].indirect(offsets))
+            zs.append(keep.tile([P, UNIT], U8, name="zs%d" % u, align_bytes=64))
+            nc.vector.tensor_copy(zs[u][:], zs_tab[:].indirect(offsets))
+
+        xw, xs, late = [], [], {}
+
+        def gather_text_words(pool, s, tag):
+            t = pool.tile([P, E * C], U32, name="xw%d" % s, tag=tag, align_bytes=64)
+            nc.vector.tensor_copy(t[:], xw_tab[s][:].indirect(list1[:]))
+            xw.append(t)
+
+        def gather_text_scales():
+            xs0 = keep.tile([P, E * C], U8, name="xs0", align_bytes=64)
+            nc.vector.tensor_copy(xs0[:], xs_tab[:].indirect(list1[:]))
+            nc.sync.dma_start(out=xs1[0 : P - 4, :].bitcast(I32), in_=xs0[4:P, :].bitcast(I32))
+            xs.extend([xs0, xs1])
+
+
+        def first_layer(u):
+            turned = pst.tile([P, 2, 2, P], F32, name="turned")
+            for j in range(2):
+                if u < E:
+                    e = u
+                    passes = [(zw[u], zs[u], j * P, wz, wz_pl, e)]
+                else:
+                    e = 2 * (u - E) + j
+                    passes = [(xw[s], xs[s], e * C, late["w1"], w1_pl, 2 * e + s) for s in range(2)]
+                pre = ps1.tile([P, H], F32, name="pre")
+                for s, (words, scales, c0, w, w_pl, g) in enumerate(passes):
+                    nc.tensor.matmul_mx(
+                        out=pre[:],
+                        lhsT=words[:, c0 : c0 + P].bitcast(FP8X4),
+                        lhsT_scale=scales[:, c0 : c0 + P],
+                        rhs=w[:, g * 2 * H : (g + 1) * 2 * H].bitcast(FP4X4),
+                        rhs_scale=w_pl[:, g * H : (g + 1) * H],
+                        start=(s == 0),
+                        stop=(s == len(passes) - 1),
+                    )
+                hid = ring.tile([P, H], BF16, name="hid", bufs=3)
+                nc.scalar.activation(
+                    out=hid[:].rearrange("p (a q c) -> p a q c", a=2, c=2),
+                    in_=pre[:].rearrange("p (q a c) -> p a q c", a=2, c=2),
+                    func=SILU,
+                )
+                pairs = hid[:].bitcast(F32)
+                for a in range(2):
+                    nc.tensor.transpose(turned[:, j, a, :], pairs[:, a * P : (a + 1) * P], ident[:])
+            grouped = ring.tile([P, 4 * UNIT], BF16, name="grouped", tag="early" if u < 2 else "late", align_bytes=64)
+            nc.scalar.copy(
+                out=grouped[:].bitcast(F32).rearrange("p (j s a) -> p j s a", j=2, a=2),
+                in_=turned[:].rearrange("p j a s -> p j s a"),
+            )
+            codes = ring.tile([P, UNIT], U32, name="codes", bufs=3, align_bytes=64)
+            scales = ring.tile([P, UNIT], U8, name="scales", bufs=3, align_bytes=64)
+            nc.vector.quantize_mx(out=codes[:].bitcast(FP8X4), scales=scales[:], in_=grouped[:])
+            return codes, scales
+
+        def second_layer(u, codes, scales):
+            if u < E:
+                parts = [(u, 0, UNIT)]
+                windows, offsets, gate = patch_out, list2[:, u * cols : (u + 1) * cols], late["g2"][:, u * UNIT : (u + 1) * UNIT]
+            else:
+                v = u - E
+                parts = [(2 * v + j, j * C, C) for j in range(2)]
+                windows, offsets, gate = text_out, list1[:, v * cols : (v + 1) * cols], late["g1"][:, v * UNIT : (v + 1) * UNIT]
+            acc = ps2.tile([P, 2 * UNIT], F32, name="acc")
+            for b in range(2):
+                for e, c0, width in parts:
+                    n0 = e * N + b * P
+                    nc.tensor.matmul_mx(
+                        out=acc[:, b * UNIT + c0 : b * UNIT + c0 + width],
+                        lhsT=w2[:, 2 * n0 : 2 * (n0 + P)].bitcast(FP4X4),
+                        lhsT_scale=w2_pl[:, n0 : n0 + P],
+                        rhs=codes[:, c0 : c0 + width].bitcast(FP8X4),
+                        rhs_scale=scales[:, c0 : c0 + width],
+                        start=True,
+                        stop=True,
+                    )
+            res = ring.tile([P, 2 * UNIT], F32, name="res", bufs=3)
+            nc.scalar.copy(out=res[:], in_=acc[:])
+            for b in range(2):
+                nc.vector.tensor_tensor(
+                    windows[b][:].indirect(offsets), res[:, b * UNIT : (b + 1) * UNIT], gate, MULT
+                )
+
+        units = E + 2
+        ahead = 2
+        made = []
+        gather_patches(0)
+        gather_patches(1)
+        for step in range(units + ahead):
+            if step < units:
+                made.append(first_layer(step))
+            if step < 2:
+                gather_patches(step + 2)
+            if step == 1:
+                late["g2"] = keep.tile([P, E * D], F32, name="g2", tag="zs_tab", align_bytes=64)
+                nc.sync.dma_start(out=late["g2"][:], in_=gate2)
+                late["w1"] = load_words("w1", "zw_tab", w1_words.rearrange("e s p c -> p (e s) c"), 2 * E, 2 * H)
+                gather_text_scales()
+                gather_text_words(ring, 0, "early")
+                gather_text_words(ring, 1, "early")
+                late["g1"] = keep.tile([P, E * C], F32, name="g1", tag="xw_tab0", align_bytes=64)
+                nc.sync.dma_start(out=late["g1"][:], in_=gate1)
+            if step >= ahead:
+                second_layer(step - ahead, *made[step - ahead])
+            if step - ahead == E - 1:
+                for b in range(2):
+                    nc.sync.dma_start(out=out[b * P : (b + 1) * P, T : T + Q], in_=patch_out[b][:])
+        for b in range(2):
+            nc.sync.dma_start(out=out[b * P : (b + 1) * P, 0:T], in_=text_out[b][:])

@@ -32,8 +32,7 @@ def tile_moe_mmo_silu_kernel(
         keep = ctx.enter_context(tc.tile_pool(name="keep", bufs=1))
         ring = ctx.enter_context(tc.tile_pool(name="ring", bufs=2))
         ps1 = ctx.enter_context(tc.psum_pool(name="ps1", bufs=4))
-        pst = ctx.enter_context(tc.psum_pool(name="pst", bufs=2))
-        ps2 = ctx.enter_context(tc.psum_pool(name="ps2", bufs=2))
+        pst = ctx.enter_context(tc.psum_pool(name="pst", bufs=1))
 
         def plane(engine, name, width):
             t = keep.tile([P, width], U8, name=name, tag=name, align_bytes=64)
@@ -59,14 +58,14 @@ def tile_moe_mmo_silu_kernel(
         wz_pl = plane(nc.vector, "wz_pl", E * H)
         xs_tab = plane(nc.vector, "xs_tab", T)
         w2_pl = plane(nc.vector, "w2_pl", E * N)
-        w1_pl = plane(nc.vector, "w1_pl", 2 * E * H)
         xs1 = plane(nc.vector, "xs1", E * C)
         text_out = [keep.tile([P, T], F32, name="text_out%d" % b) for b in range(2)]
+        w1_pl = plane(nc.vector, "w1_pl", 2 * E * H)
+        for b in range(2):
+            nc.vector.memset(text_out[b][:], 0.0)
         patch_out = [keep.tile([P, Q], F32, name="patch_out%d" % b) for b in range(2)]
         ident = keep.tile([P, P], F32, name="ident")
         make_identity(nc, ident[:])
-        for b in range(2):
-            nc.gpsimd.memset(text_out[b][:], 0.0)
 
         list2 = keep.tile([P, E * D // PER_COL], U16, name="list2")
         nc.sync.dma_start(list2[:], offs2)
@@ -77,18 +76,25 @@ def tile_moe_mmo_silu_kernel(
         list1 = keep.tile([P, E * C // PER_COL], U16, name="list1")
         nc.sync.dma_start(list1[:], offs)
         load_scale_rows(nc.sync, wz_pl, wz_scales.rearrange("e s b i -> b (e s) i"))
-        xw_tab = [keep.tile([P, T], U32, name="xw_tab%d" % s, tag="xw_tab%d" % s, align_bytes=64) for s in range(2)]
-        for s in range(2):
+        xw_tab = []
+
+        def load_text_words(s):
+            xw_tab.append(keep.tile([P, T], U32, name="xw_tab", tag="xw_tab%d" % s, align_bytes=64))
             nc.sync.dma_start(
                 out=xw_tab[s][:].bitcast(I32), in_=x_words[s].rearrange("p t d -> p (t d)").bitcast(I32)
             )
-        w2 = load_words("w2", "w2", w2_words.rearrange("e s p c -> p (e s) c"), E, 2 * N)
+
+        load_text_words(0)
         for q in range(4):
             nc.sync.dma_start(
                 out=xs_tab[32 * q : 32 * q + 8, :].bitcast(I32),
                 in_=x_scales[:, 4 * q : 4 * q + 4, :].bitcast(I32),
             )
+        load_text_words(1)
+        w2 = load_words("w2", "w2", w2_words.rearrange("e s p c -> p (e s) c"), E, 2 * N)
         load_scale_rows(nc.sync, w2_pl, w2_scales.rearrange("e s b n -> b (e s) n"))
+        g2 = keep.tile([P, E * D], F32, name="g2")
+        nc.sync.dma_start(out=g2[:], in_=gate2)
         load_scale_rows(nc.sync, w1_pl, w1_scales.rearrange("e s b i -> b (e s) i"))
 
         cols = UNIT // PER_COL
@@ -116,7 +122,7 @@ def tile_moe_mmo_silu_kernel(
 
 
         def first_layer(u):
-            turned = pst.tile([P, 2, 2, P], F32, name="turned")
+            turned = pst.tile([P, 2, 2, P], F32, name="turned", tag="bank%d" % (u % 3))
             for j in range(2):
                 if u < E:
                     e = u
@@ -135,7 +141,7 @@ def tile_moe_mmo_silu_kernel(
                         start=(s == 0),
                         stop=(s == len(passes) - 1),
                     )
-                hid = ring.tile([P, H], BF16, name="hid", bufs=3)
+                hid = ring.tile([P, H], BF16, name="hid", bufs=4)
                 nc.scalar.activation(
                     out=hid[:].rearrange("p (a q c) -> p a q c", a=2, c=2),
                     in_=pre[:].rearrange("p (q a c) -> p a q c", a=2, c=2),
@@ -144,66 +150,67 @@ def tile_moe_mmo_silu_kernel(
                 pairs = hid[:].bitcast(F32)
                 for a in range(2):
                     nc.tensor.transpose(turned[:, j, a, :], pairs[:, a * P : (a + 1) * P], ident[:])
-            grouped = ring.tile([P, 4 * UNIT], BF16, name="grouped", tag="early" if u < 2 else "late", align_bytes=64)
+            if u < 2:
+                grouped = keep.tile([P, 4 * UNIT], BF16, name="grouped", tag="grouped%d" % u, align_bytes=64)
+            else:
+                grouped = ring.tile([P, 4 * UNIT], BF16, name="grouped", align_bytes=64)
             nc.scalar.copy(
                 out=grouped[:].bitcast(F32).rearrange("p (j s a) -> p j s a", j=2, a=2),
                 in_=turned[:].rearrange("p j a s -> p j s a"),
             )
-            codes = ring.tile([P, UNIT], U32, name="codes", bufs=3, align_bytes=64)
+            if u < 2:
+                codes = keep.tile([P, UNIT], U32, name="codes", tag="xw_tab%d" % u, align_bytes=64)
+            else:
+                codes = ring.tile([P, UNIT], U32, name="codes", bufs=3, align_bytes=64)
             scales = ring.tile([P, UNIT], U8, name="scales", bufs=3, align_bytes=64)
             nc.vector.quantize_mx(out=codes[:].bitcast(FP8X4), scales=scales[:], in_=grouped[:])
             return codes, scales
 
-        def second_layer(u, codes, scales):
+        def second_layer(u, b, codes, scales):
             if u < E:
                 parts = [(u, 0, UNIT)]
-                windows, offsets, gate = patch_out, list2[:, u * cols : (u + 1) * cols], late["g2"][:, u * UNIT : (u + 1) * UNIT]
+            else:
+                parts = [(2 * (u - E) + j, j * C, C) for j in range(2)]
+            acc = pst.tile([P, UNIT], F32, name="acc", tag="bank%d" % ((u + 1) % 3 if b else 3))
+            for e, c0, width in parts:
+                n0 = e * N + b * P
+                nc.tensor.matmul_mx(
+                    out=acc[:, c0 : c0 + width],
+                    lhsT=w2[:, 2 * n0 : 2 * (n0 + P)].bitcast(FP4X4),
+                    lhsT_scale=w2_pl[:, n0 : n0 + P],
+                    rhs=codes[:, c0 : c0 + width].bitcast(FP8X4),
+                    rhs_scale=scales[:, c0 : c0 + width],
+                    start=True,
+                    stop=True,
+                )
+            res = ring.tile([P, UNIT], F32, name="res", bufs=4)
+            nc.scalar.copy(out=res[:], in_=acc[:])
+            if u < E:
+                window, offsets, gate = patch_out[b], list2[:, u * cols : (u + 1) * cols], g2[:, u * UNIT : (u + 1) * UNIT]
             else:
                 v = u - E
-                parts = [(2 * v + j, j * C, C) for j in range(2)]
-                windows, offsets, gate = text_out, list1[:, v * cols : (v + 1) * cols], late["g1"][:, v * UNIT : (v + 1) * UNIT]
-            acc = ps2.tile([P, 2 * UNIT], F32, name="acc")
-            for b in range(2):
-                for e, c0, width in parts:
-                    n0 = e * N + b * P
-                    nc.tensor.matmul_mx(
-                        out=acc[:, b * UNIT + c0 : b * UNIT + c0 + width],
-                        lhsT=w2[:, 2 * n0 : 2 * (n0 + P)].bitcast(FP4X4),
-                        lhsT_scale=w2_pl[:, n0 : n0 + P],
-                        rhs=codes[:, c0 : c0 + width].bitcast(FP8X4),
-                        rhs_scale=scales[:, c0 : c0 + width],
-                        start=True,
-                        stop=True,
-                    )
-            res = ring.tile([P, 2 * UNIT], F32, name="res", bufs=3)
-            nc.scalar.copy(out=res[:], in_=acc[:])
-            for b in range(2):
-                nc.vector.tensor_tensor(
-                    windows[b][:].indirect(offsets), res[:, b * UNIT : (b + 1) * UNIT], gate, MULT
-                )
+                window, offsets, gate = text_out[b], list1[:, v * cols : (v + 1) * cols], late["g1"][:, v * UNIT : (v + 1) * UNIT]
+            nc.vector.tensor_tensor(window[:].indirect(offsets), res[:], gate, MULT)
 
         units = E + 2
-        ahead = 2
-        made = []
         gather_patches(0)
         gather_patches(1)
-        for step in range(units + ahead):
-            if step < units:
-                made.append(first_layer(step))
-            if step < 2:
-                gather_patches(step + 2)
-            if step == 1:
-                late["g2"] = keep.tile([P, E * D], F32, name="g2", tag="zs_tab", align_bytes=64)
-                nc.sync.dma_start(out=late["g2"][:], in_=gate2)
+        gather_text_words(keep, 0, "xw0")
+        quantised = first_layer(0)
+        gather_patches(2)
+        gather_text_words(keep, 1, "grouped0")
+        for u in range(units):
+            second_layer(u, 0, *quantised)
+            ahead = first_layer(u + 1) if u + 1 < units else None
+            if u == 0:
+                gather_patches(3)
                 late["w1"] = load_words("w1", "zw_tab", w1_words.rearrange("e s p c -> p (e s) c"), 2 * E, 2 * H)
                 gather_text_scales()
-                gather_text_words(ring, 0, "early")
-                gather_text_words(ring, 1, "early")
-                late["g1"] = keep.tile([P, E * C], F32, name="g1", tag="xw_tab0", align_bytes=64)
+                late["g1"] = keep.tile([P, E * C], F32, name="g1", tag="grouped1", align_bytes=64)
                 nc.sync.dma_start(out=late["g1"][:], in_=gate1)
-            if step >= ahead:
-                second_layer(step - ahead, *made[step - ahead])
-            if step - ahead == E - 1:
+            second_layer(u, 1, *quantised)
+            quantised = ahead
+            if u == E - 1:
                 for b in range(2):
                     nc.sync.dma_start(out=out[b * P : (b + 1) * P, T : T + Q], in_=patch_out[b][:])
         for b in range(2):

from contextlib import ExitStack

import concourse.mybir as mybir
from concourse.masks import make_identity

K, L, T, Q, E, C, D = 1024, 512, 768, 1024, 4, 128, 256
H, N = 512, 256
FLOPS = 2 * E * (C * K * H + D * L * H + (C + D) * H * N)

F32 = mybir.dt.float32
BF16 = mybir.dt.bfloat16
I32 = mybir.dt.int32
U32 = mybir.dt.uint32
U16 = mybir.dt.uint16
U8 = mybir.dt.uint8
FP8X4 = mybir.dt.float8_e4m3fn_x4
FP4X4 = mybir.dt.float4_e2m1fn_x4
SILU = mybir.ActivationFunctionType.Silu
MULT = mybir.AluOpType.mult

P = 128
UNIT = 256
PER_COL = 16


def tile_moe_mmo_silu_kernel(
    tc, x_words, x_scales, z_words, z_scales, w1_words, w1_scales, wz_words, wz_scales,
    w2_words, w2_scales, gate1, gate2, offs, offs2, out,
):
    nc = tc.nc
    with ExitStack() as ctx:
        keep = ctx.enter_context(tc.tile_pool(name="keep", bufs=1))
        ring = ctx.enter_context(tc.tile_pool(name="ring", bufs=2))
        ps1 = ctx.enter_context(tc.psum_pool(name="ps1", bufs=4))
        pst = ctx.enter_context(tc.psum_pool(name="pst", bufs=1))

        def plane(engine, name, width):
            t = keep.tile([P, width], U8, name=name, tag=name, align_bytes=64)
            engine.memset(t[:].bitcast(I32), 0)
            return t

        def load_scale_rows(queue, t, rows):
            groups = rows.shape[1]
            for q in range(4):
                queue.dma_start(
                    out=t[32 * q : 32 * q + 4, :].bitcast(I32).rearrange("p (g c) -> p g c", g=groups),
                    in_=rows[4 * q : 4 * q + 4, :, :].bitcast(I32),
                )

        def load_words(name, tag, src, groups, width):
            t = keep.tile([P, groups * width], U8, name=name, tag=tag, align_bytes=64)
            nc.sync.dma_start(
                out=t[:].bitcast(I32).rearrange("p (g c) -> p g c", g=groups), in_=src.bitcast(I32)
            )
            return t

        zs_tab = plane(nc.gpsimd, "zs_tab", Q)
        wz_pl = plane(nc.vector, "wz_pl", E * H)
        xs_tab = plane(nc.vector, "xs_tab", T)
        w2_pl = plane(nc.vector, "w2_pl", E * N)
        xs1 = plane(nc.vector, "xs1", E * C)
        text_out = [keep.tile([P, T], F32, name="text_out%d" % b) for b in range(2)]
        w1_pl = plane(nc.vector, "w1_pl", 2 * E * H)
        for b in range(2):
            nc.vector.memset(text_out[b][:], 0.0)
        patch_out = [keep.tile([P, Q], F32, name="patch_out%d" % b) for b in range(2)]
        ident = keep.tile([P, P], F32, name="ident")
        make_identity(nc, ident[:])

        list2 = keep.tile([P, E * D // PER_COL], U16, name="list2")
        nc.sync.dma_start(list2[:], offs2)
        zw_tab = keep.tile([P, Q], U32, name="zw_tab", tag="zw_tab", align_bytes=64)
        nc.sync.dma_start(out=zw_tab[:].bitcast(I32), in_=z_words[0].rearrange("p t d -> p (t d)").bitcast(I32))
        load_scale_rows(nc.sync, zs_tab, z_scales.rearrange("s b t -> b s t"))
        wz = load_words("wz", "wz", wz_words.rearrange("e s p c -> p (e s) c"), E, 2 * H)
        list1 = keep.tile([P, E * C // PER_COL], U16, name="list1")
        nc.sync.dma_start(list1[:], offs)
        load_scale_rows(nc.sync, wz_pl, wz_scales.rearrange("e s b i -> b (e s) i"))
        xw_tab = []

        def load_text_words(s):
            xw_tab.append(keep.tile([P, T], U32, name="xw_tab", tag="xw_tab%d" % s, align_bytes=64))
            nc.sync.dma_start(
                out=xw_tab[s][:].bitcast(I32), in_=x_words[s].rearrange("p t d -> p (t d)").bitcast(I32)
            )

        load_text_words(0)
        for q in range(4):
            nc.sync.dma_start(
                out=xs_tab[32 * q : 32 * q + 8, :].bitcast(I32),
                in_=x_scales[:, 4 * q : 4 * q + 4, :].bitcast(I32),
            )
        load_text_words(1)
        w2 = load_words("w2", "w2", w2_words.rearrange("e s p c -> p (e s) c"), E, 2 * N)
        load_scale_rows(nc.sync, w2_pl, w2_scales.rearrange("e s b n -> b (e s) n"))
        g2 = keep.tile([P, E * D], F32, name="g2")
        nc.sync.dma_start(out=g2[:], in_=gate2)
        load_scale_rows(nc.sync, w1_pl, w1_scales.rearrange("e s b i -> b (e s) i"))

        cols = UNIT // PER_COL
        zw, zs = [], []

        def gather_patches(u):
            offsets = list2[:, u * cols : (u + 1) * cols]
            zw.append(ring.tile([P, UNIT], U32, name="zw", align_bytes=64))
            nc.vector.tensor_copy(zw[u][:], zw_tab[:].indirect(offsets))
            zs.append(keep.tile([P, UNIT], U8, name="zs%d" % u, align_bytes=64))
            nc.vector.tensor_copy(zs[u][:], zs_tab[:].indirect(offsets))

        xw, xs, late = [], [], {}

        def gather_text_words(pool, s, tag):
            t = pool.tile([P, E * C], U32, name="xw%d" % s, tag=tag, align_bytes=64)
            nc.vector.tensor_copy(t[:], xw_tab[s][:].indirect(list1[:]))
            xw.append(t)

        def gather_text_scales():
            xs0 = keep.tile([P, E * C], U8, name="xs0", align_bytes=64)
            nc.vector.tensor_copy(xs0[:], xs_tab[:].indirect(list1[:]))
            nc.sync.dma_start(out=xs1[0 : P - 4, :].bitcast(I32), in_=xs0[4:P, :].bitcast(I32))
            xs.extend([xs0, xs1])


        def first_layer(u):
            turned = pst.tile([P, 2, 2, P], F32, name="turned", tag="bank%d" % (u % 3))
            for j in range(2):
                if u < E:
                    e = u
                    passes = [(zw[u], zs[u], j * P, wz, wz_pl, e)]
                else:
                    e = 2 * (u - E) + j
                    passes = [(xw[s], xs[s], e * C, late["w1"], w1_pl, 2 * e + s) for s in range(2)]
                pre = ps1.tile([P, H], F32, name="pre")
                for s, (words, scales, c0, w, w_pl, g) in enumerate(passes):
                    nc.tensor.matmul_mx(
                        out=pre[:],
                        lhsT=words[:, c0 : c0 + P].bitcast(FP8X4),
                        lhsT_scale=scales[:, c0 : c0 + P],
                        rhs=w[:, g * 2 * H : (g + 1) * 2 * H].bitcast(FP4X4),
                        rhs_scale=w_pl[:, g * H : (g + 1) * H],
                        start=(s == 0),
                        stop=(s == len(passes) - 1),
                    )
                hid = ring.tile([P, H], BF16, name="hid", bufs=4)
                nc.scalar.activation(
                    out=hid[:].rearrange("p (a q c) -> p a q c", a=2, c=2),
                    in_=pre[:].rearrange("p (q a c) -> p a q c", a=2, c=2),
                    func=SILU,
                )
                pairs = hid[:].bitcast(F32)
                for a in range(2):
                    nc.tensor.transpose(turned[:, j, a, :], pairs[:, a * P : (a + 1) * P], ident[:])
            if u < 2:
                grouped = keep.tile([P, 4 * UNIT], BF16, name="grouped", tag="grouped%d" % u, align_bytes=64)
            else:
                grouped = ring.tile([P, 4 * UNIT], BF16, name="grouped", align_bytes=64)
            nc.scalar.copy(
                out=grouped[:].bitcast(F32).rearrange("p (j s a) -> p j s a", j=2, a=2),
                in_=turned[:].rearrange("p j a s -> p j s a"),
            )
            if u < 2:
                codes = keep.tile([P, UNIT], U32, name="codes", tag="xw_tab%d" % u, align_bytes=64)
            else:
                codes = ring.tile([P, UNIT], U32, name="codes", bufs=3, align_bytes=64)
            scales = ring.tile([P, UNIT], U8, name="scales", bufs=3, align_bytes=64)
            nc.vector.quantize_mx(out=codes[:].bitcast(FP8X4), scales=scales[:], in_=grouped[:])
            return codes, scales

        def second_layer(u, b, codes, scales):
            if u < E:
                parts = [(u, 0, UNIT)]
            else:
                parts = [(2 * (u - E) + j, j * C, C) for j in range(2)]
            acc = pst.tile([P, UNIT], F32, name="acc", tag="bank%d" % ((u + 1) % 3 if b else 3))
            for e, c0, width in parts:
                n0 = e * N + b * P
                nc.tensor.matmul_mx(
                    out=acc[:, c0 : c0 + width],
                    lhsT=w2[:, 2 * n0 : 2 * (n0 + P)].bitcast(FP4X4),
                    lhsT_scale=w2_pl[:, n0 : n0 + P],
                    rhs=codes[:, c0 : c0 + width].bitcast(FP8X4),
                    rhs_scale=scales[:, c0 : c0 + width],
                    start=True,
                    stop=True,
                )
            res = ring.tile([P, UNIT], F32, name="res", bufs=4)
            nc.scalar.copy(out=res[:], in_=acc[:])
            if u < E:
                window, offsets, gate = patch_out[b], list2[:, u * cols : (u + 1) * cols], g2[:, u * UNIT : (u + 1) * UNIT]
            else:
                v = u - E
                window, offsets, gate = text_out[b], list1[:, v * cols : (v + 1) * cols], late["g1"][:, v * UNIT : (v + 1) * UNIT]
            nc.vector.tensor_tensor(window[:].indirect(offsets), res[:], gate, MULT)

        units = E + 2
        gather_patches(0)
        gather_patches(1)
        gather_text_words(keep, 0, "xw0")
        quantised = first_layer(0)
        gather_patches(2)
        gather_text_words(keep, 1, "grouped0")
        for u in range(units):
            second_layer(u, 0, *quantised)
            ahead = first_layer(u + 1) if u + 1 < units else None
            if u == 0:
                gather_patches(3)
                late["w1"] = load_words("w1", "zw_tab", w1_words.rearrange("e s p c -> p (e s) c"), 2 * E, 2 * H)
                gather_text_scales()
                late["g1"] = keep.tile([P, E * C], F32, name="g1", tag="grouped1", align_bytes=64)
                nc.sync.dma_start(out=late["g1"][:], in_=gate1)
            second_layer(u, 1, *quantised)
            quantised = ahead
            if u == E - 1:
                for b in range(2):
                    nc.sync.dma_start(out=out[b * P : (b + 1) * P, T : T + Q], in_=patch_out[b][:])
        for b in range(2):
            nc.sync.dma_start(out=out[b * P : (b + 1) * P, 0:T], in_=text_out[b][:])
